import numpy as np, ml_dtypes
CORES = [10,18,34,42,58,66,82,90,98,106]
N = 10
TK = 512
def setup_inputs(rng):
    return {"x": rng.standard_normal((N, 128, TK), dtype=np.float32).astype(ml_dtypes.bfloat16), "w": rng.standard_normal((N, 128, 128), dtype=np.float32).astype(ml_dtypes.bfloat16)}
def setup_inputs_big(rng):
    d = setup_inputs(rng)
    for k in ("x", "w"): d[k] = (d[k].astype(np.float32) * 1024.0).astype(d[k].dtype)
    return d
def setup_inputs_small(rng):
    d = setup_inputs(rng)
    for k in ("x", "w"): d[k] = (d[k].astype(np.float32) * (1 / 1024.0)).astype(d[k].dtype)
    return d
def setup_inputs_apart(rng):
    d = setup_inputs(rng)
    f = (10.0 ** rng.permutation(np.linspace(-1.5, 1.5, N))).astype(np.float32).reshape(N, 1, 1)
    for k in ("x", "w"): d[k] = (d[k].astype(np.float32) * f).astype(d[k].dtype)
    return d
def setup_inputs_neg(rng):
    d = setup_inputs(rng)
    d["x"] = (np.abs(d["x"].astype(np.float32)) * 1048576.0).astype(d["x"].dtype); d["w"] = (-np.abs(d["w"].astype(np.float32))).astype(d["w"].dtype)
    return d
def reference(x, w):
    X, W = x.astype(np.float64), w.astype(np.float64)
    y = np.stack([np.max([W[j].T @ X[r] for j in range(N)], axis=0) for r in range(N)])
    return {"y": y.astype(ml_dtypes.bfloat16)}

@@ -1,0 +1,111 @@
+from concourse.bass import DstId, RemoteDMATransfer
+from concourse.mybir import AluOpType
+
+N = 10
+TK = 512
+M = 128
+NBANK = 8
+NJOB = N + 1
+
+SCRATCH = {
+    "xs": ("sbuf", [128, TK], "bfloat16"),
+    "wall": ("sbuf", [128, N * M], "bfloat16"),
+    "acc0": ("sbuf", [128, TK], "bfloat16"),
+    "acc1": ("sbuf", [128, TK], "bfloat16"),
+}
+for _b in range(NBANK):
+    SCRATCH["ps%d" % _b] = ("psum", [128, TK], "float32")
+
+SEMAPHORES = (["wl", "xl", "sent", "sta", "stb"] + ["arr%d" % j for j in range(N)]
+              + ["mm%d" % i for i in range(NJOB)] + ["vd%d" % i for i in range(NJOB)])
+
+
+def rounds(T, topo):
+    chips = [topo.chip(c) for c in T.cores]
+    pa = [r for r in range(N) if chips[r] == chips[0] or topo.same_plane(chips[r], chips[0])]
+    pb = [r for r in range(N) if r not in pa]
+    send = [[] for _ in range(N)]
+    recv = [[] for _ in range(N)]
+
+    def put(a, b):
+        send[a].append(b)
+        recv[b].append(a)
+
+    for s in range(max(len(pa), len(pb))):
+        for i, a in enumerate(pa):
+            if s < len(pb):
+                put(a, pb[(i + s) % len(pb)])
+        for i, b in enumerate(pb):
+            if s < len(pa):
+                put(b, pa[(i + s + 1) % len(pa)])
+    for s in range(1, max(len(pa), len(pb))):
+        for grp in (pa, pb):
+            for i, a in enumerate(grp):
+                if s < len(grp):
+                    put(a, grp[(i + s) % len(grp)])
+    return send, recv
+
+
+def rank_program(g, core, T, topo):
+    r = T.rank_of(core)
+    if r is None:
+        return
+    send, recv = rounds(T, topo)
+
+    def slot(j):
+        return T.wall[:, j * M:(j + 1) * M]
+
+    g.sync.dma_start(slot(r), T.w[:, :]).then_inc(T.sem.wl, 16)
+    g.sync.dma_start(T.xs[:, :], T.x[:, :]).then_inc(T.sem.xl, 16)
+
+    mask = topo.mask(core, T.cores[send[r][0]])
+    for d in send[r]:
+        mask &= topo.mask(core, T.cores[d])
+    neng = bin(mask).count("1")
+    ids = []
+    for d in send[r]:
+        rid, pid, _se = topo.addr(T.cores[d])
+        ids.append(DstId(rid=rid, pnc=pid))
+    g.wait_ge(T.sem.wl, 16)
+    g.remote_dma_fused(
+        [RemoteDMATransfer(dst_ids=ids, dma_engine_mask=mask, remote_sem=T.sem["arr%d" % r],
+                           srcs=[slot(r)], dsts=[slot(r) for _ in send[r]], alu_op=0)],
+        local_sem=T.sem.sent)
+
+    order = [r] + recv[r]
+    jobs = [(j, 0, TK) for j in order[:-1]] + [(order[-1], 0, TK // 2), (order[-1], TK // 2, TK)]
+    accs = [T.acc0, T.acc1]
+
+    g.tensor.wait_ge(T.sem.wl, 16)
+    g.tensor.wait_ge(T.sem.xl, 16)
+    seen = {r}
+    for i, (j, c0, c1) in enumerate(jobs):
+        if j not in seen:
+            g.tensor.wait_ge(T.sem["arr%d" % j], neng)
+            seen.add(j)
+        if i >= NBANK:
+            g.tensor.wait_ge(T.sem["vd%d" % (i - NBANK)], 1)
+        ps = T["ps%d" % (i % NBANK)]
+        g.tensor.matmul(ps[:, c0:c1], slot(j), T.xs[:, c0:c1], True, True).then_inc(T.sem["mm%d" % i], 1)
+
+    nfull = len(jobs) - 2
+    for i, (j, c0, c1) in enumerate(jobs):
+        ps = T["ps%d" % (i % NBANK)]
+        g.vector.wait_ge(T.sem["mm%d" % i], 1)
+        if i == 0:
+            g.vector.tensor_copy(accs[0][:, :], ps[:, :]).then_inc(T.sem.vd0, 1)
+            continue
+        k = min(i, nfull)
+        g.vector.wait_ge(T.sem["vd%d" % (i - 1)], 1)
+        g.vector.tensor_tensor(accs[k % 2][:, c0:c1], ps[:, c0:c1], accs[(k - 1) % 2][:, c0:c1],
+                               AluOpType.max).then_inc(T.sem["vd%d" % i], 1)
+
+    out = accs[nfull % 2]
+    h = TK // 2
+    g.sync.wait_ge(T.sem["vd%d" % (NJOB - 2)], 1)
+    g.sync.dma_start(T.y[:, 0:h], out[:, 0:h]).then_inc(T.sem.sta, 16)
+    g.scalar.wait_ge(T.sem["vd%d" % (NJOB - 1)], 1)
+    g.scalar.dma_start(T.y[:, h:TK], out[:, h:TK]).then_inc(T.sem.stb, 16)
+    g.sync.wait_ge(T.sem.sta, 16)
+    g.scalar.wait_ge(T.sem.stb, 16)
+    g.wait_ge(T.sem.sent, neng)

@@ -5,9 +5,13 @@ N = 10
 TK = 512
 M = 128
 NBANK = 8
-NJOB = N + 1
+NJOB = 2 * N
+CUT = 160
+NDIRECT = 8
+EXPECT = [0, 1, 2, 3, 4, 5, 6, 8, 7]
 
 SCRATCH = {
+    "wd": ("dram", [128, M], "bfloat16"),
     "xs": ("sbuf", [128, TK], "bfloat16"),
     "wall": ("sbuf", [128, N * M], "bfloat16"),
     "acc0": ("sbuf", [128, TK], "bfloat16"),
@@ -16,7 +20,7 @@ SCRATCH = {
 for _b in range(NBANK):
     SCRATCH["ps%d" % _b] = ("psum", [128, TK], "float32")
 
-SEMAPHORES = (["wl", "xl", "sent", "sta", "stb"] + ["arr%d" % j for j in range(N)]
+SEMAPHORES = (["wc", "wl", "xl", "sent", "hin", "sta", "stb"] + ["arr%d" % j for j in range(N)]
               + ["mm%d" % i for i in range(NJOB)] + ["vd%d" % i for i in range(NJOB)])
 
 
@@ -46,40 +50,71 @@ def rounds(T, topo):
     return send, recv
 
 
+def helper_of(rc, T, topo):
+    return [c for c in range(topo.CORES_PER_CHIP * topo.CHIPS)
+            if topo.chip(c) == topo.chip(rc) and c not in T.cores and topo.die(c) != topo.die(rc)
+            and all(topo.may_write(c, d) for d in T.cores)][0]
+
+
+def nbits(m):
+    return bin(m).count("1")
+
+
 def rank_program(g, core, T, topo):
-    r = T.rank_of(core)
-    if r is None:
-        return
     send, recv = rounds(T, topo)
 
     def slot(j):
         return T.wall[:, j * M:(j + 1) * M]
 
+    def spread(j, ranks_to):
+        mask = topo.mask(core, T.cores[ranks_to[0]])
+        ids = []
+        for d in ranks_to:
+            mask &= topo.mask(core, T.cores[d])
+            rid, pid, _se = topo.addr(T.cores[d])
+            ids.append(DstId(rid=rid, pnc=pid))
+        g.remote_dma_fused(
+            [RemoteDMATransfer(dst_ids=ids, dma_engine_mask=mask, remote_sem=T.sem["arr%d" % j],
+                               srcs=[T.wd[:, :]], dsts=[slot(j) for _ in ranks_to], alu_op=0)],
+            local_sem=T.sem.sent)
+        return nbits(mask)
+
+    def home_mask(rc, hc):
+        return topo.mask(rc, hc) & ~topo.mask(rc, [c for c in T.cores if c != rc][0])
+
+    r = T.rank_of(core)
+    if r is None:
+        for j, rc in enumerate(T.cores):
+            if helper_of(rc, T, topo) == core:
+                g.wait_ge(T.sem.hin, nbits(home_mask(rc, core)))
+                n = spread(j, send[j][NDIRECT:])
+                g.wait_ge(T.sem.sent, n)
+        return
+
+    g.sync.dma_start(T.wd[:, :], T.w[:, :]).then_inc(T.sem.wc, 16)
     g.sync.dma_start(slot(r), T.w[:, :]).then_inc(T.sem.wl, 16)
     g.sync.dma_start(T.xs[:, :], T.x[:, :]).then_inc(T.sem.xl, 16)
 
-    mask = topo.mask(core, T.cores[send[r][0]])
-    for d in send[r]:
-        mask &= topo.mask(core, T.cores[d])
-    neng = bin(mask).count("1")
-    ids = []
-    for d in send[r]:
-        rid, pid, _se = topo.addr(T.cores[d])
-        ids.append(DstId(rid=rid, pnc=pid))
-    g.wait_ge(T.sem.wl, 16)
-    g.remote_dma_fused(
-        [RemoteDMATransfer(dst_ids=ids, dma_engine_mask=mask, remote_sem=T.sem["arr%d" % r],
-                           srcs=[slot(r)], dsts=[slot(r) for _ in send[r]], alu_op=0)],
-        local_sem=T.sem.sent)
+    hc = helper_of(core, T, topo)
+    home = home_mask(core, hc)
+    hrid, hpid, _hse = topo.addr(hc)
+    g.wait_ge(T.sem.wc, 16)
+    neng = spread(r, send[r][:NDIRECT])
+    g.remote_dma(out_ap=T.wd[:, :], in_ap=T.wd[:, :], remote_sem=T.sem.hin, local_sem=T.sem.sent,
+                 pid=hpid, routing_id=hrid, dma_engine_mask=home)
 
-    order = [r] + recv[r]
-    jobs = [(j, 0, TK) for j in order[:-1]] + [(order[-1], 0, TK // 2), (order[-1], TK // 2, TK)]
+    order = [r] + [recv[r][k] for k in EXPECT]
+    jobs = []
+    for p, j in enumerate(order):
+        cut = CUT if p == N - 1 else TK // 2
+        jobs.append((p, j, 0, cut))
+        jobs.append((p, j, cut, TK))
     accs = [T.acc0, T.acc1]
 
     g.tensor.wait_ge(T.sem.wl, 16)
     g.tensor.wait_ge(T.sem.xl, 16)
     seen = {r}
-    for i, (j, c0, c1) in enumerate(jobs):
+    for i, (p, j, c0, c1) in enumerate(jobs):
         if j not in seen:
             g.tensor.wait_ge(T.sem["arr%d" % j], neng)
             seen.add(j)
@@ -88,24 +123,21 @@ def rank_program(g, core, T, topo):
         ps = T["ps%d" % (i % NBANK)]
         g.tensor.matmul(ps[:, c0:c1], slot(j), T.xs[:, c0:c1], True, True).then_inc(T.sem["mm%d" % i], 1)
 
-    nfull = len(jobs) - 2
-    for i, (j, c0, c1) in enumerate(jobs):
+    for i, (p, j, c0, c1) in enumerate(jobs):
         ps = T["ps%d" % (i % NBANK)]
         g.vector.wait_ge(T.sem["mm%d" % i], 1)
-        if i == 0:
-            g.vector.tensor_copy(accs[0][:, :], ps[:, :]).then_inc(T.sem.vd0, 1)
+        if p == 0:
+            g.vector.tensor_copy(accs[0][:, c0:c1], ps[:, c0:c1]).then_inc(T.sem["vd%d" % i], 1)
             continue
-        k = min(i, nfull)
-        g.vector.wait_ge(T.sem["vd%d" % (i - 1)], 1)
-        g.vector.tensor_tensor(accs[k % 2][:, c0:c1], ps[:, c0:c1], accs[(k - 1) % 2][:, c0:c1],
+        g.vector.wait_ge(T.sem["vd%d" % (i - 2)], 1)
+        g.vector.tensor_tensor(accs[p % 2][:, c0:c1], ps[:, c0:c1], accs[(p - 1) % 2][:, c0:c1],
                                AluOpType.max).then_inc(T.sem["vd%d" % i], 1)
 
-    out = accs[nfull % 2]
-    h = TK // 2
+    out = accs[(N - 1) % 2]
     g.sync.wait_ge(T.sem["vd%d" % (NJOB - 2)], 1)
-    g.sync.dma_start(T.y[:, 0:h], out[:, 0:h]).then_inc(T.sem.sta, 16)
+    g.sync.dma_start(T.y[:, 0:CUT], out[:, 0:CUT]).then_inc(T.sem.sta, 16)
     g.scalar.wait_ge(T.sem["vd%d" % (NJOB - 1)], 1)
-    g.scalar.dma_start(T.y[:, h:TK], out[:, h:TK]).then_inc(T.sem.stb, 16)
+    g.scalar.dma_start(T.y[:, CUT:TK], out[:, CUT:TK]).then_inc(T.sem.stb, 16)
     g.sync.wait_ge(T.sem.sta, 16)
     g.scalar.wait_ge(T.sem.stb, 16)
-    g.wait_ge(T.sem.sent, neng)
+    g.wait_ge(T.sem.sent, neng + nbits(home))

from concourse.bass import DstId, RemoteDMATransfer
from concourse.mybir import AluOpType

N = 10
TK = 512
M = 128
NBANK = 8
NJOB = 2 * N
CUT = 160
NDIRECT = 8
EXPECT = [0, 1, 2, 3, 4, 5, 6, 8, 7]

SCRATCH = {
    "wd": ("dram", [128, M], "bfloat16"),
    "xs": ("sbuf", [128, TK], "bfloat16"),
    "wall": ("sbuf", [128, N * M], "bfloat16"),
    "acc0": ("sbuf", [128, TK], "bfloat16"),
    "acc1": ("sbuf", [128, TK], "bfloat16"),
}
for _b in range(NBANK):
    SCRATCH["ps%d" % _b] = ("psum", [128, TK], "float32")

SEMAPHORES = (["wc", "wl", "xl", "sent", "hin", "sta", "stb"] + ["arr%d" % j for j in range(N)]
              + ["mm%d" % i for i in range(NJOB)] + ["vd%d" % i for i in range(NJOB)])


def rounds(T, topo):
    chips = [topo.chip(c) for c in T.cores]
    pa = [r for r in range(N) if chips[r] == chips[0] or topo.same_plane(chips[r], chips[0])]
    pb = [r for r in range(N) if r not in pa]
    send = [[] for _ in range(N)]
    recv = [[] for _ in range(N)]

    def put(a, b):
        send[a].append(b)
        recv[b].append(a)

    for s in range(max(len(pa), len(pb))):
        for i, a in enumerate(pa):
            if s < len(pb):
                put(a, pb[(i + s) % len(pb)])
        for i, b in enumerate(pb):
            if s < len(pa):
                put(b, pa[(i + s + 1) % len(pa)])
    for s in range(1, max(len(pa), len(pb))):
        for grp in (pa, pb):
            for i, a in enumerate(grp):
                if s < len(grp):
                    put(a, grp[(i + s) % len(grp)])
    return send, recv


def helper_of(rc, T, topo):
    return [c for c in range(topo.CORES_PER_CHIP * topo.CHIPS)
            if topo.chip(c) == topo.chip(rc) and c not in T.cores and topo.die(c) != topo.die(rc)
            and all(topo.may_write(c, d) for d in T.cores)][0]


def nbits(m):
    return bin(m).count("1")


def rank_program(g, core, T, topo):
    send, recv = rounds(T, topo)

    def slot(j):
        return T.wall[:, j * M:(j + 1) * M]

    def spread(j, ranks_to):
        mask = topo.mask(core, T.cores[ranks_to[0]])
        ids = []
        for d in ranks_to:
            mask &= topo.mask(core, T.cores[d])
            rid, pid, _se = topo.addr(T.cores[d])
            ids.append(DstId(rid=rid, pnc=pid))
        g.remote_dma_fused(
            [RemoteDMATransfer(dst_ids=ids, dma_engine_mask=mask, remote_sem=T.sem["arr%d" % j],
                               srcs=[T.wd[:, :]], dsts=[slot(j) for _ in ranks_to], alu_op=0)],
            local_sem=T.sem.sent)
        return nbits(mask)

    def home_mask(rc, hc):
        return topo.mask(rc, hc) & ~topo.mask(rc, [c for c in T.cores if c != rc][0])

    r = T.rank_of(core)
    if r is None:
        for j, rc in enumerate(T.cores):
            if helper_of(rc, T, topo) == core:
                g.wait_ge(T.sem.hin, nbits(home_mask(rc, core)))
                n = spread(j, send[j][NDIRECT:])
                g.wait_ge(T.sem.sent, n)
        return

    g.sync.dma_start(T.wd[:, :], T.w[:, :]).then_inc(T.sem.wc, 16)
    g.sync.dma_start(slot(r), T.w[:, :]).then_inc(T.sem.wl, 16)
    g.sync.dma_start(T.xs[:, :], T.x[:, :]).then_inc(T.sem.xl, 16)

    hc = helper_of(core, T, topo)
    home = home_mask(core, hc)
    hrid, hpid, _hse = topo.addr(hc)
    g.wait_ge(T.sem.wc, 16)
    neng = spread(r, send[r][:NDIRECT])
    g.remote_dma(out_ap=T.wd[:, :], in_ap=T.wd[:, :], remote_sem=T.sem.hin, local_sem=T.sem.sent,
                 pid=hpid, routing_id=hrid, dma_engine_mask=home)

    order = [r] + [recv[r][k] for k in EXPECT]
    jobs = []
    for p, j in enumerate(order):
        cut = CUT if p == N - 1 else TK // 2
        jobs.append((p, j, 0, cut))
        jobs.append((p, j, cut, TK))
    accs = [T.acc0, T.acc1]

    g.tensor.wait_ge(T.sem.wl, 16)
    g.tensor.wait_ge(T.sem.xl, 16)
    seen = {r}
    for i, (p, j, c0, c1) in enumerate(jobs):
        if j not in seen:
            g.tensor.wait_ge(T.sem["arr%d" % j], neng)
            seen.add(j)
        if i >= NBANK:
            g.tensor.wait_ge(T.sem["vd%d" % (i - NBANK)], 1)
        ps = T["ps%d" % (i % NBANK)]
        g.tensor.matmul(ps[:, c0:c1], slot(j), T.xs[:, c0:c1], True, True).then_inc(T.sem["mm%d" % i], 1)

    for i, (p, j, c0, c1) in enumerate(jobs):
        ps = T["ps%d" % (i % NBANK)]
        g.vector.wait_ge(T.sem["mm%d" % i], 1)
        if p == 0:
            g.vector.tensor_copy(accs[0][:, c0:c1], ps[:, c0:c1]).then_inc(T.sem["vd%d" % i], 1)
            continue
        g.vector.wait_ge(T.sem["vd%d" % (i - 2)], 1)
        g.vector.tensor_tensor(accs[p % 2][:, c0:c1], ps[:, c0:c1], accs[(p - 1) % 2][:, c0:c1],
                               AluOpType.max).then_inc(T.sem["vd%d" % i], 1)

    out = accs[(N - 1) % 2]
    g.sync.wait_ge(T.sem["vd%d" % (NJOB - 2)], 1)
    g.sync.dma_start(T.y[:, 0:CUT], out[:, 0:CUT]).then_inc(T.sem.sta, 16)
    g.scalar.wait_ge(T.sem["vd%d" % (NJOB - 1)], 1)
    g.scalar.dma_start(T.y[:, CUT:TK], out[:, CUT:TK]).then_inc(T.sem.stb, 16)
    g.sync.wait_ge(T.sem.sta, 16)
    g.scalar.wait_ge(T.sem.stb, 16)
    g.wait_ge(T.sem.sent, neng + nbits(home))
